import numpy as np
import ml_dtypes


def mxq(x, axis, fmt="e4m3"):
    dtype, down = {"e4m3": (ml_dtypes.float8_e4m3fn, 7), "e5m2": (ml_dtypes.float8_e5m2, 14)}[fmt]
    v = np.moveaxis(np.asarray(x, np.float32).astype(ml_dtypes.bfloat16).astype(np.float64), axis, -1)
    blocks = v.reshape(v.shape[:-1] + (-1, 32))
    amax = np.abs(blocks).max(-1, keepdims=True)
    byte = np.maximum(np.where(amax > 0, np.frexp(amax)[1] - 1 + 127, 0) - down, 1)
    scale = np.exp2(byte - 127.0)
    codes = (blocks / scale).astype(np.float32).astype(dtype).astype(np.float64)
    return np.moveaxis((codes * scale).reshape(v.shape), -1, axis)


WIDE = False


def mx_kscale(k):
    if not WIDE:
        return np.ones(k)
    levels = np.array([10, -10, 5, -5, 0])
    if k % 512:
        return np.exp2(np.random.permutation(np.resize(levels, k // 32))).repeat(32)
    a = np.empty((k // 512, 16))
    for p in range(k // 512):
        a[p, :8] = np.random.permutation(np.resize(levels, 8))
        for g in range(8):
            far = levels[np.abs(levels - a[p, g]) >= 10]
            a[p, g + 8] = far[np.random.randint(len(far))]
    return np.exp2(a.ravel()).repeat(32)


def f64(x):
    return np.asarray(x).astype(np.float64)


def striped(idx):
    return np.tile(idx.reshape(-1, 16).T, (8, 1)).astype(np.uint16)


def unstriped(offs):
    return offs[:16].T.reshape(-1).astype(np.int64)


E2M1 = np.array([0.0, 0.5, 1.0, 1.5, 2.0, 3.0, 4.0, 6.0, -0.0, -0.5, -1.0, -1.5, -2.0, -3.0, -4.0, -6.0])


def pack_weight(w, fmt):
    k, n = w.shape
    w = f64(np.asarray(w, np.float32).astype(ml_dtypes.bfloat16)).reshape(k // 32, 32, n)
    amax = np.abs(w).max(1)
    if fmt == "e4m3":
        byte = np.frexp(amax)[1] - 1 + 127 - 7
    else:
        mant, ex = np.frexp(amax / 6.0)
        byte = np.where(mant > 0.5, ex, ex - 1) + 127
    byte = np.clip(np.where(amax > 0, byte, 1), 1, 254)
    scaled = (w * np.exp2(127.0 - byte)[:, None, :]).reshape(k, n).astype(np.float32)
    by_word = np.ascontiguousarray(scaled.reshape(k // 512, 128, 4, n).transpose(0, 1, 3, 2))
    if fmt == "e4m3":
        words = by_word.astype(ml_dtypes.float8_e4m3fn).view(np.uint8)
    else:
        c = by_word.astype(ml_dtypes.float4_e2m1fn).view(np.uint8) & 0xF
        words = (c[..., 0::2] | (c[..., 1::2] << 4)).reshape(k // 512, 128, 2 * n)
    return np.ascontiguousarray(words), np.ascontiguousarray(byte.astype(np.uint8).reshape(k // 512, 16, n))


def unpack_weight(words, scales, fmt):
    g, _, n = scales.shape
    words = np.ascontiguousarray(words).reshape(g, 128, n, -1)
    if fmt == "e4m3":
        vals = words.view(ml_dtypes.float8_e4m3fn).astype(np.float64)
    else:
        nib = np.empty((g, 128, n, 4), np.uint8)
        nib[..., 0::2] = words & 0xF
        nib[..., 1::2] = words >> 4
        vals = E2M1[nib]
    vals = vals * np.repeat(np.exp2(scales.astype(np.float64) - 127.0), 8, axis=1)[..., None]
    return vals.transpose(0, 1, 3, 2).reshape(g * 512, n)


def gelu(v):
    return 0.5 * v * (1.0 + np.tanh(np.sqrt(2.0 / np.pi) * (v + 0.044715 * v**3)))


K, H, T, S, P = 1536, 512, 4096, 1024, 512


def setup_inputs():
    n = np.random.standard_normal
    s = mx_kscale(K)[:, None]
    u = mx_kscale(H)[:, None]
    tab_words, tab_scales = pack_weight(n((K, T)) * s, "e4m3")
    w1 = 0.85 * n((K, H)) / np.sqrt(K) / s
    w4_words, w4_scales = pack_weight(0.85 * n((K, H)) / np.sqrt(K) / s, "e2m1")
    w3_words, w3_scales = pack_weight(1.3 * n((H, H)) / np.sqrt(H) / u, "e4m3")
    perm = np.random.permutation(S)
    return {
        "tab_words": tab_words, "tab_scales": tab_scales,
        "offs": striped(np.random.permutation(T)[:S]),
        "pos1": striped(perm[:P]),
        "pos2": striped(perm[P:]),
        "w1": w1.astype(np.float32),
        "w4_words": w4_words, "w4_scales": w4_scales,
        "thr": n(H).astype(np.float32),
        "lay": (2.5 * n((H, P))).astype(np.float32),
        "skip": np.random.uniform(0.5, 1.5, H).astype(np.float32),
        "wgs": np.exp(0.3 * n((128, P))).astype(np.float32),
        "gain": (np.random.uniform(0.6, 1.6, H) * u[:, 0]).astype(np.float32),
        "w3_words": w3_words, "w3_scales": w3_scales,
    }


def reference(tab_words, tab_scales, offs, pos1, pos2, w1, w4_words, w4_scales,
              thr, lay, skip, wgs, gain, w3_words, w3_scales):
    v = unpack_weight(tab_words, tab_scales, "e4m3")[:, unstriped(offs)]
    w4 = unpack_weight(w4_words, w4_scales, "e2m1")
    w3 = unpack_weight(w3_words, w3_scales, "e4m3")
    h = np.minimum(mxq(f64(w1), 0, "e4m3").T @ v, w4.T @ v)
    a = 1.0 / (1.0 + np.exp(-(h[:, unstriped(pos1)] + f64(thr)[:, None])))
    a = a * f64(lay)
    page = f64(skip)[:, None] * h
    page[:, unstriped(pos2)] = np.tile(f64(wgs), (H // 128, 1)) * a
    q = mxq(page * f64(gain)[:, None], 0, "e4m3")
    return (w3.T @ q) + h

@@ -1,0 +1,244 @@
+from contextlib import ExitStack
+
+import concourse.mybir as mybir
+
+K, H, T, S, NP = 1536, 512, 4096, 1024, 512
+FLOPS = 2 * (2 * K * H * S + H * H * S)
+
+F32 = mybir.dt.float32
+BF16 = mybir.dt.bfloat16
+I32 = mybir.dt.int32
+U32 = mybir.dt.uint32
+U16 = mybir.dt.uint16
+U8 = mybir.dt.uint8
+E4M3 = mybir.dt.float8_e4m3fn_x4
+E2M1 = mybir.dt.float4_e2m1fn_x4
+ALU = mybir.AluOpType
+ACT = mybir.ActivationFunctionType
+
+P = 128
+PACK = 4
+K_PASS = P * PACK
+PASSES = K // K_PASS
+BANK = 512
+HALVES = S // BANK
+QUADS = 4
+QUAD = 32
+
+
+def tile_list_felt_lane_readout_kernel(
+    tc, tab_words, tab_scales, offs, pos1, pos2, w1, w4_words, w4_scales,
+    thr, lay, skip, wgs, gain, w3_words, w3_scales, out,
+):
+    nc = tc.nc
+    with ExitStack() as ctx:
+        lists = ctx.enter_context(tc.tile_pool(name="lists", bufs=1))
+        keep = ctx.enter_context(tc.tile_pool(name="keep", bufs=1))
+        psum = ctx.enter_context(tc.psum_pool(name="psum", bufs=1))
+
+        def held(name, shape, dtype):
+            return keep.tile(shape, dtype, name=name, align_bytes=64)
+
+        def half(hf):
+            return slice(hf * BANK, (hf + 1) * BANK)
+
+        def bank(t, hf):
+            return psum.tile([P, BANK], F32, name=f"bank{t}{hf}", tag=f"bank{t}{hf}")
+
+        def staged(t, hf):
+            return keep.tile([P, BANK], F32, name=f"staged{t}{hf}", tag=f"staged{t}{hf}")
+
+        offs_t = lists.tile([P, S // 16], U16, name="offs_t")
+        pos1_t = lists.tile([P, NP // 16], U16, name="pos1_t")
+        pos2_t = lists.tile([P, NP // 16], U16, name="pos2_t")
+
+        tab = [held(f"tab{a}", [P, T], I32) for a in range(PASSES)]
+        tab_sc = held("tab_sc", [P, T], U8)
+        w4_raw = held("w4_raw", [P, PASSES, H // 2], I32)
+        w3_raw = held("w3_raw", [P, H], I32)
+        w4s_raw = held("w4s_raw", [P, PASSES, H], U8)
+        w3s_raw = held("w3s_raw", [P, H], U8)
+        w1_raw = [held(f"w1_raw{a}", [P, PACK, H], F32) for a in range(PASSES)]
+        wgs_t = held("wgs_t", [P, PACK, NP], F32)
+        lay_t = [held(f"lay{t}", [P, NP], F32) for t in range(PACK)]
+        thr_t = held("thr_t", [P, PACK], F32)
+        skip_t = held("skip_t", [P, PACK], F32)
+        gain_t = held("gain_t", [P, PACK], F32)
+        picked_sc = held("picked_sc", [P, S], U8)
+        v_sc = [held(f"v_sc{a}", [P, S], U8) for a in range(PASSES)]
+
+        nc.gpsimd.memset(w4s_raw[:].rearrange("p a c -> p (a c)").bitcast(I32), 0)
+        nc.vector.memset(tab_sc[32:64, :].bitcast(I32), 0)
+        nc.vector.memset(tab_sc[64:112, :].bitcast(I32), 0)
+        nc.gpsimd.memset(w3s_raw[:].bitcast(I32), 0)
+        for plane in v_sc:
+            nc.gpsimd.memset(plane[:].bitcast(I32), 0)
+
+        sc_rows = tab_scales.rearrange("a q t -> (a q) t").bitcast(I32)
+        nc.sync.dma_start(tab_sc[0:32, :].bitcast(I32), sc_rows[0:32])
+        nc.sync.dma_start(tab_sc[112:128, :].bitcast(I32), sc_rows[32:48])
+        nc.sync.dma_start(offs_t[:], offs)
+        nc.sync.dma_start(w4_raw[:], w4_words.rearrange("a p b -> p a b").bitcast(I32))
+        words = [tab_words[a].rearrange("p t i -> p (t i)").bitcast(I32) for a in range(PASSES)]
+        nc.sync.dma_start(tab[0][:, :T // 2], words[0][:, :T // 2])
+        for q in range(QUADS):
+            nc.sync.dma_start(
+                w4s_raw[QUAD * q:QUAD * q + 4].bitcast(I32),
+                w4_scales[:, 4 * q:4 * q + 4, :].rearrange("a r c -> r a c").bitcast(I32))
+        nc.sync.dma_start(tab[0][:, T // 2:], words[0][:, T // 2:])
+        nc.sync.dma_start(tab[1][:], words[1])
+        nc.sync.dma_start(w3_raw[:], w3_words[0].rearrange("p c i -> p (c i)").bitcast(I32))
+        for q in range(QUADS):
+            nc.sync.dma_start(
+                w3s_raw[QUAD * q:QUAD * q + 4, :].bitcast(I32),
+                w3_scales[0, 4 * q:4 * q + 4, :].bitcast(I32))
+        nc.sync.dma_start(tab[2][:], words[2])
+        for a in range(PASSES):
+            rows = w1[a * K_PASS:(a + 1) * K_PASS, :]
+            nc.sync.dma_start(w1_raw[a][:], rows.rearrange("(p j) c -> p j c", j=PACK))
+        nc.sync.dma_start(pos1_t[:], pos1)
+        nc.sync.dma_start(pos2_t[:], pos2)
+        for q in range(QUADS):
+            nc.sync.dma_start(wgs_t[QUAD * q:QUAD * (q + 1)], wgs.rearrange("(v t) m -> v t m", t=PACK))
+        for t in range(PACK):
+            nc.sync.dma_start(lay_t[t][:], lay.rearrange("(p t) m -> t p m", t=PACK)[t])
+        for vec, tile in ((thr, thr_t), (skip, skip_t), (gain, gain_t)):
+            nc.gpsimd.dma_start(tile[:], vec.rearrange("(p t) -> p t", t=PACK))
+
+        nc.vector.tensor_copy(picked_sc[:], tab_sc[:].indirect(offs_t[:]))
+        for a, first in enumerate((0, 16, 112)):
+            for q in range(QUADS):
+                nc.gpsimd.dma_start(
+                    v_sc[a][QUAD * q:QUAD * q + 4, :].bitcast(I32),
+                    picked_sc[first + 4 * q:first + 4 * q + 4, :].bitcast(I32))
+
+        w4 = held("w4", [P, PASSES, 2 * H], U8)
+        nc.vector.tensor_copy(
+            out=w4[:].bitcast(U16).rearrange("p a (t m) -> p a m t", t=PACK),
+            in_=w4_raw[:].bitcast(U16).rearrange("p a (m t) -> p a m t", t=PACK))
+
+        v = [[held(f"v{a}{hf}", [P, BANK], U32) for hf in range(HALVES)] for a in range(PASSES)]
+
+        def gather_words(a):
+            for hf in range(HALVES):
+                cols = BANK // 16
+                nc.vector.tensor_copy(
+                    v[a][hf][:], tab[a][:].bitcast(U32).indirect(offs_t[:, hf * cols:(hf + 1) * cols]))
+
+        w4s = held("w4s", [P, PASSES, H], U8)
+        nc.vector.tensor_copy(
+            out=w4s[:].rearrange("p a (t m) -> p a m t", t=PACK),
+            in_=w4s_raw[:].rearrange("p a (m t) -> p a m t", t=PACK))
+        gather_words(0)
+        gather_words(1)
+        w3 = held("w3", [P, H], I32)
+        w3s = held("w3s", [P, H], U8)
+        nc.vector.tensor_copy(
+            out=w3[:].rearrange("p (t m) -> p m t", t=PACK),
+            in_=w3_raw[:].rearrange("p (m t) -> p m t", t=PACK))
+        nc.vector.tensor_copy(
+            out=w3s[:].rearrange("p (t m) -> p m t", t=PACK),
+            in_=w3s_raw[:].rearrange("p (m t) -> p m t", t=PACK))
+        gather_words(2)
+
+        order = [(t, hf) for t in range(PACK) for hf in range(HALVES)]
+
+        sum4 = {key: bank(*key) for key in order}
+        for a in range(PASSES):
+            for t, hf in order:
+                nc.tensor.matmul_mx(
+                    out=sum4[t, hf][:],
+                    lhsT=w4[:, a, 2 * P * t:2 * P * (t + 1)].bitcast(E2M1),
+                    lhsT_scale=w4s[:, a, P * t:P * (t + 1)],
+                    rhs=v[a][hf][:].bitcast(E4M3),
+                    rhs_scale=v_sc[a][:, half(hf)],
+                    start=(a == 0), stop=(a == PASSES - 1))
+        read4 = {key: staged(*key) for key in order}
+        for key in order:
+            nc.scalar.copy(out=read4[key][:], in_=sum4[key][:])
+
+        w1_bf = [held(f"w1_bf{a}", [P, PACK * H], BF16) for a in range(PASSES)]
+        w1_q = [held(f"w1_q{a}", [P, H], U32) for a in range(PASSES)]
+        w1_sc = [held(f"w1_sc{a}", [P, H], U8) for a in range(PASSES)]
+        for a in range(PASSES):
+            nc.vector.tensor_copy(
+                out=w1_bf[a][:].rearrange("p (t m j) -> p m j t", t=PACK, j=PACK),
+                in_=w1_raw[a][:].rearrange("p j (m t) -> p m j t", t=PACK))
+            pieces = 1 if a < PASSES - 1 else 2
+            width = H // pieces
+            for c in range(0, H, width):
+                nc.vector.quantize_mx(
+                    out=w1_q[a][:, c:c + width].bitcast(E4M3),
+                    scales=w1_sc[a][:, c:c + width],
+                    in_=w1_bf[a][:, PACK * c:PACK * (c + width)])
+
+        sum1 = {key: bank(*key) for key in order}
+
+        def w1_pass(a, t, hf):
+            nc.tensor.matmul_mx(
+                out=sum1[t, hf][:],
+                lhsT=w1_q[a][:, P * t:P * (t + 1)].bitcast(E4M3),
+                lhsT_scale=w1_sc[a][:, P * t:P * (t + 1)],
+                rhs=v[a][hf][:].bitcast(E4M3),
+                rhs_scale=v_sc[a][:, half(hf)],
+                start=(a == 0), stop=(a == PASSES - 1))
+
+        for t, hf in order:
+            w1_pass(0, t, hf)
+        for step in range(PACK + 1):
+            for hf in range(HALVES):
+                if step == 0:
+                    w1_pass(1, 0, hf)
+                if step + 1 < PACK:
+                    w1_pass(1, step + 1, hf)
+            for hf in range(HALVES):
+                if step < PACK:
+                    w1_pass(2, step, hf)
+
+        h = [held(f"h{t}", [P, S], F32) for t in range(PACK)]
+        for t, hf in order:
+            nc.vector.tensor_tensor(h[t][:, half(hf)], sum1[t, hf][:], read4[t, hf][:], ALU.min)
+
+        weight = [held(f"weight{t}", [P, NP], F32) for t in range(PACK)]
+        for t in range(PACK):
+            nc.gpsimd.tensor_tensor(weight[t][:], lay_t[t][:], wgs_t[:, t, :], ALU.mult)
+
+        look = [held(f"look{t}", [P, NP], F32) for t in range(PACK)]
+        page = [held(f"page{t}", [P, S], F32) for t in range(PACK)]
+        for t in range(PACK):
+            nc.scalar.activation(
+                out=look[t][:], in_=h[t][:].indirect(pos1_t[:]), func=ACT.Sigmoid, bias=thr_t[:, t:t + 1])
+            nc.scalar.activation(out=page[t][:], in_=h[t][:], func=ACT.Copy, scale=skip_t[:, t:t + 1])
+
+        page_bf = [held(f"page_bf{hf}", [P, BANK, PACK], BF16) for hf in range(HALVES)]
+        for t in range(PACK):
+            nc.vector.tensor_tensor(page[t][:].indirect(pos2_t[:]), look[t][:], weight[t][:], ALU.mult)
+            for hf in range(HALVES):
+                if hf == 0 and t >= 2:
+                    nc.vector.tensor_scalar(
+                        page_bf[hf][:, :, t], page[t][:, half(hf)], gain_t[:, t:t + 1], None, ALU.mult)
+                else:
+                    nc.scalar.activation(
+                        out=page_bf[hf][:, :, t], in_=page[t][:, half(hf)], func=ACT.Copy,
+                        scale=gain_t[:, t:t + 1])
+
+        out_rows = out.rearrange("(p t) j -> t p j", t=PACK)
+        page_q = [held(f"page_q{hf}", [P, BANK], U32) for hf in range(HALVES)]
+        page_sc = [held(f"page_sc{hf}", [P, BANK], U8) for hf in range(HALVES)]
+        for hf in range(HALVES):
+            nc.vector.quantize_mx(
+                out=page_q[hf][:].bitcast(E4M3), scales=page_sc[hf][:],
+                in_=page_bf[hf][:].rearrange("p c t -> p (c t)"))
+        for hf in range(HALVES):
+            for t in range(PACK):
+                acc = bank(t, hf)
+                nc.tensor.matmul_mx(
+                    out=acc[:],
+                    lhsT=w3[:, P * t:P * (t + 1)].bitcast(E4M3),
+                    lhsT_scale=w3s[:, P * t:P * (t + 1)],
+                    rhs=page_q[hf][:].bitcast(E4M3),
+                    rhs_scale=page_sc[hf][:],
+                    start=True, stop=True)
+                result = staged(t, hf)
+                nc.vector.tensor_tensor(result[:], acc[:], h[t][:, half(hf)], ALU.add)
+                nc.sync.dma_start(out_rows[t][:, half(hf)], result[:])

@@ -34,6 +34,7 @@ def tile_list_felt_lane_readout_kernel(
     with ExitStack() as ctx:
         lists = ctx.enter_context(tc.tile_pool(name="lists", bufs=1))
         keep = ctx.enter_context(tc.tile_pool(name="keep", bufs=1))
+        reused = ctx.enter_context(tc.tile_pool(name="reused", bufs=1))
         psum = ctx.enter_context(tc.psum_pool(name="psum", bufs=1))
 
         def held(name, shape, dtype):
@@ -52,15 +53,18 @@ def tile_list_felt_lane_readout_kernel(
         pos1_t = lists.tile([P, NP // 16], U16, name="pos1_t")
         pos2_t = lists.tile([P, NP // 16], U16, name="pos2_t")
 
-        tab = [held(f"tab{a}", [P, T], I32) for a in range(PASSES)]
+        def placed(name, shape, dtype, offset):
+            return reused.tile(shape, dtype, name=name, offset=offset)
+
+        tab = [placed(f"tab{a}", [P, T], I32, 4 * T * a) for a in range(PASSES)]
         tab_sc = held("tab_sc", [P, T], U8)
         w4_raw = held("w4_raw", [P, PASSES, H // 2], I32)
         w3_raw = held("w3_raw", [P, H], I32)
         w4s_raw = held("w4s_raw", [P, PASSES, H], U8)
         w3s_raw = held("w3s_raw", [P, H], U8)
-        w1_raw = [held(f"w1_raw{a}", [P, PACK, H], F32) for a in range(PASSES)]
-        wgs_t = held("wgs_t", [P, PACK, NP], F32)
-        lay_t = [held(f"lay{t}", [P, NP], F32) for t in range(PACK)]
+        w1_raw = [placed(f"w1_raw{a}", [P, PACK, H], F32, 4 * T * a) for a in range(PASSES)]
+        wgs_t = placed("wgs_t", [P, PACK, NP], F32, 4 * T * 2 + 2 * T)
+        lay_t = [placed(f"lay{t}", [P, NP], F32, 4 * NP * t) for t in range(PACK)]
         thr_t = held("thr_t", [P, PACK], F32)
         skip_t = held("skip_t", [P, PACK], F32)
         gain_t = held("gain_t", [P, PACK], F32)
@@ -80,35 +84,27 @@ def tile_list_felt_lane_readout_kernel(
         nc.sync.dma_start(offs_t[:], offs)
         nc.sync.dma_start(w4_raw[:], w4_words.rearrange("a p b -> p a b").bitcast(I32))
         words = [tab_words[a].rearrange("p t i -> p (t i)").bitcast(I32) for a in range(PASSES)]
-        nc.sync.dma_start(tab[0][:, :T // 2], words[0][:, :T // 2])
+        nc.sync.dma_start(tab[0][:], words[0])
         for q in range(QUADS):
             nc.sync.dma_start(
                 w4s_raw[QUAD * q:QUAD * q + 4].bitcast(I32),
                 w4_scales[:, 4 * q:4 * q + 4, :].rearrange("a r c -> r a c").bitcast(I32))
-        nc.sync.dma_start(tab[0][:, T // 2:], words[0][:, T // 2:])
         nc.sync.dma_start(tab[1][:], words[1])
-        nc.sync.dma_start(w3_raw[:], w3_words[0].rearrange("p c i -> p (c i)").bitcast(I32))
-        for q in range(QUADS):
-            nc.sync.dma_start(
-                w3s_raw[QUAD * q:QUAD * q + 4, :].bitcast(I32),
-                w3_scales[0, 4 * q:4 * q + 4, :].bitcast(I32))
-        nc.sync.dma_start(tab[2][:], words[2])
-        for a in range(PASSES):
-            rows = w1[a * K_PASS:(a + 1) * K_PASS, :]
-            nc.sync.dma_start(w1_raw[a][:], rows.rearrange("(p j) c -> p j c", j=PACK))
         nc.sync.dma_start(pos1_t[:], pos1)
         nc.sync.dma_start(pos2_t[:], pos2)
+        nc.sync.dma_start(w3_raw[:], w3_words[0].rearrange("p c i -> p (c i)").bitcast(I32))
+        nc.sync.dma_start(tab[2][:], words[2])
         for q in range(QUADS):
-            nc.sync.dma_start(wgs_t[QUAD * q:QUAD * (q + 1)], wgs.rearrange("(v t) m -> v t m", t=PACK))
-        for t in range(PACK):
-            nc.sync.dma_start(lay_t[t][:], lay.rearrange("(p t) m -> t p m", t=PACK)[t])
+            nc.gpsimd.dma_start(
+                w3s_raw[QUAD * q:QUAD * q + 4, :].bitcast(I32),
+                w3_scales[0, 4 * q:4 * q + 4, :].bitcast(I32))
         for vec, tile in ((thr, thr_t), (skip, skip_t), (gain, gain_t)):
             nc.gpsimd.dma_start(tile[:], vec.rearrange("(p t) -> p t", t=PACK))
 
         nc.vector.tensor_copy(picked_sc[:], tab_sc[:].indirect(offs_t[:]))
         for a, first in enumerate((0, 16, 112)):
             for q in range(QUADS):
-                nc.gpsimd.dma_start(
+                nc.scalar.dma_start(
                     v_sc[a][QUAD * q:QUAD * q + 4, :].bitcast(I32),
                     picked_sc[first + 4 * q:first + 4 * q + 4, :].bitcast(I32))
 
@@ -124,6 +120,8 @@ def tile_list_felt_lane_readout_kernel(
                 cols = BANK // 16
                 nc.vector.tensor_copy(
                     v[a][hf][:], tab[a][:].bitcast(U32).indirect(offs_t[:, hf * cols:(hf + 1) * cols]))
+            rows = w1[a * K_PASS:(a + 1) * K_PASS, :]
+            nc.sync.dma_start(w1_raw[a][:], rows.rearrange("(p j) c -> p j c", j=PACK))
 
         w4s = held("w4s", [P, PASSES, H], U8)
         nc.vector.tensor_copy(
@@ -140,6 +138,8 @@ def tile_list_felt_lane_readout_kernel(
             out=w3s[:].rearrange("p (t m) -> p m t", t=PACK),
             in_=w3s_raw[:].rearrange("p (m t) -> p m t", t=PACK))
         gather_words(2)
+        for q in range(QUADS):
+            nc.sync.dma_start(wgs_t[QUAD * q:QUAD * (q + 1)], wgs.rearrange("(v t) m -> v t m", t=PACK))
 
         order = [(t, hf) for t in range(PACK) for hf in range(HALVES)]
 
@@ -164,6 +164,9 @@ def tile_list_felt_lane_readout_kernel(
             nc.vector.tensor_copy(
                 out=w1_bf[a][:].rearrange("p (t m j) -> p m j t", t=PACK, j=PACK),
                 in_=w1_raw[a][:].rearrange("p j (m t) -> p m j t", t=PACK))
+            if a == 0:
+                for t in range(PACK):
+                    nc.sync.dma_start(lay_t[t][:], lay.rearrange("(p t) m -> t p m", t=PACK)[t])
             pieces = 1 if a < PASSES - 1 else 2
             width = H // pieces
             for c in range(0, H, width):

from contextlib import ExitStack

import concourse.mybir as mybir

K, H, T, S, NP = 1536, 512, 4096, 1024, 512
FLOPS = 2 * (2 * K * H * S + H * H * S)

F32 = mybir.dt.float32
BF16 = mybir.dt.bfloat16
I32 = mybir.dt.int32
U32 = mybir.dt.uint32
U16 = mybir.dt.uint16
U8 = mybir.dt.uint8
E4M3 = mybir.dt.float8_e4m3fn_x4
E2M1 = mybir.dt.float4_e2m1fn_x4
ALU = mybir.AluOpType
ACT = mybir.ActivationFunctionType

P = 128
PACK = 4
K_PASS = P * PACK
PASSES = K // K_PASS
BANK = 512
HALVES = S // BANK
QUADS = 4
QUAD = 32


def tile_list_felt_lane_readout_kernel(
    tc, tab_words, tab_scales, offs, pos1, pos2, w1, w4_words, w4_scales,
    thr, lay, skip, wgs, gain, w3_words, w3_scales, out,
):
    nc = tc.nc
    with ExitStack() as ctx:
        lists = ctx.enter_context(tc.tile_pool(name="lists", bufs=1))
        keep = ctx.enter_context(tc.tile_pool(name="keep", bufs=1))
        reused = ctx.enter_context(tc.tile_pool(name="reused", bufs=1))
        psum = ctx.enter_context(tc.psum_pool(name="psum", bufs=1))

        def held(name, shape, dtype):
            return keep.tile(shape, dtype, name=name, align_bytes=64)

        def half(hf):
            return slice(hf * BANK, (hf + 1) * BANK)

        def bank(t, hf):
            return psum.tile([P, BANK], F32, name=f"bank{t}{hf}", tag=f"bank{t}{hf}")

        def staged(t, hf):
            return keep.tile([P, BANK], F32, name=f"staged{t}{hf}", tag=f"staged{t}{hf}")

        offs_t = lists.tile([P, S // 16], U16, name="offs_t")
        pos1_t = lists.tile([P, NP // 16], U16, name="pos1_t")
        pos2_t = lists.tile([P, NP // 16], U16, name="pos2_t")

        def placed(name, shape, dtype, offset):
            return reused.tile(shape, dtype, name=name, offset=offset)

        tab = [placed(f"tab{a}", [P, T], I32, 4 * T * a) for a in range(PASSES)]
        tab_sc = held("tab_sc", [P, T], U8)
        w4_raw = held("w4_raw", [P, PASSES, H // 2], I32)
        w3_raw = held("w3_raw", [P, H], I32)
        w4s_raw = held("w4s_raw", [P, PASSES, H], U8)
        w3s_raw = held("w3s_raw", [P, H], U8)
        w1_raw = [placed(f"w1_raw{a}", [P, PACK, H], F32, 4 * T * a) for a in range(PASSES)]
        wgs_t = placed("wgs_t", [P, PACK, NP], F32, 4 * T * 2 + 2 * T)
        lay_t = [placed(f"lay{t}", [P, NP], F32, 4 * NP * t) for t in range(PACK)]
        thr_t = held("thr_t", [P, PACK], F32)
        skip_t = held("skip_t", [P, PACK], F32)
        gain_t = held("gain_t", [P, PACK], F32)
        picked_sc = held("picked_sc", [P, S], U8)
        v_sc = [held(f"v_sc{a}", [P, S], U8) for a in range(PASSES)]

        nc.gpsimd.memset(w4s_raw[:].rearrange("p a c -> p (a c)").bitcast(I32), 0)
        nc.vector.memset(tab_sc[32:64, :].bitcast(I32), 0)
        nc.vector.memset(tab_sc[64:112, :].bitcast(I32), 0)
        nc.gpsimd.memset(w3s_raw[:].bitcast(I32), 0)
        for plane in v_sc:
            nc.gpsimd.memset(plane[:].bitcast(I32), 0)

        sc_rows = tab_scales.rearrange("a q t -> (a q) t").bitcast(I32)
        nc.sync.dma_start(tab_sc[0:32, :].bitcast(I32), sc_rows[0:32])
        nc.sync.dma_start(tab_sc[112:128, :].bitcast(I32), sc_rows[32:48])
        nc.sync.dma_start(offs_t[:], offs)
        nc.sync.dma_start(w4_raw[:], w4_words.rearrange("a p b -> p a b").bitcast(I32))
        words = [tab_words[a].rearrange("p t i -> p (t i)").bitcast(I32) for a in range(PASSES)]
        nc.sync.dma_start(tab[0][:], words[0])
        for q in range(QUADS):
            nc.sync.dma_start(
                w4s_raw[QUAD * q:QUAD * q + 4].bitcast(I32),
                w4_scales[:, 4 * q:4 * q + 4, :].rearrange("a r c -> r a c").bitcast(I32))
        nc.sync.dma_start(tab[1][:], words[1])
        nc.sync.dma_start(pos1_t[:], pos1)
        nc.sync.dma_start(pos2_t[:], pos2)
        nc.sync.dma_start(w3_raw[:], w3_words[0].rearrange("p c i -> p (c i)").bitcast(I32))
        nc.sync.dma_start(tab[2][:], words[2])
        for q in range(QUADS):
            nc.gpsimd.dma_start(
                w3s_raw[QUAD * q:QUAD * q + 4, :].bitcast(I32),
                w3_scales[0, 4 * q:4 * q + 4, :].bitcast(I32))
        for vec, tile in ((thr, thr_t), (skip, skip_t), (gain, gain_t)):
            nc.gpsimd.dma_start(tile[:], vec.rearrange("(p t) -> p t", t=PACK))

        nc.vector.tensor_copy(picked_sc[:], tab_sc[:].indirect(offs_t[:]))
        for a, first in enumerate((0, 16, 112)):
            for q in range(QUADS):
                nc.scalar.dma_start(
                    v_sc[a][QUAD * q:QUAD * q + 4, :].bitcast(I32),
                    picked_sc[first + 4 * q:first + 4 * q + 4, :].bitcast(I32))

        w4 = held("w4", [P, PASSES, 2 * H], U8)
        nc.vector.tensor_copy(
            out=w4[:].bitcast(U16).rearrange("p a (t m) -> p a m t", t=PACK),
            in_=w4_raw[:].bitcast(U16).rearrange("p a (m t) -> p a m t", t=PACK))

        v = [[held(f"v{a}{hf}", [P, BANK], U32) for hf in range(HALVES)] for a in range(PASSES)]

        def gather_words(a):
            for hf in range(HALVES):
                cols = BANK // 16
                nc.vector.tensor_copy(
                    v[a][hf][:], tab[a][:].bitcast(U32).indirect(offs_t[:, hf * cols:(hf + 1) * cols]))
            rows = w1[a * K_PASS:(a + 1) * K_PASS, :]
            nc.sync.dma_start(w1_raw[a][:], rows.rearrange("(p j) c -> p j c", j=PACK))

        w4s = held("w4s", [P, PASSES, H], U8)
        nc.vector.tensor_copy(
            out=w4s[:].rearrange("p a (t m) -> p a m t", t=PACK),
            in_=w4s_raw[:].rearrange("p a (m t) -> p a m t", t=PACK))
        gather_words(0)
        gather_words(1)
        w3 = held("w3", [P, H], I32)
        w3s = held("w3s", [P, H], U8)
        nc.vector.tensor_copy(
            out=w3[:].rearrange("p (t m) -> p m t", t=PACK),
            in_=w3_raw[:].rearrange("p (m t) -> p m t", t=PACK))
        nc.vector.tensor_copy(
            out=w3s[:].rearrange("p (t m) -> p m t", t=PACK),
            in_=w3s_raw[:].rearrange("p (m t) -> p m t", t=PACK))
        gather_words(2)
        for q in range(QUADS):
            nc.sync.dma_start(wgs_t[QUAD * q:QUAD * (q + 1)], wgs.rearrange("(v t) m -> v t m", t=PACK))

        order = [(t, hf) for t in range(PACK) for hf in range(HALVES)]

        sum4 = {key: bank(*key) for key in order}
        for a in range(PASSES):
            for t, hf in order:
                nc.tensor.matmul_mx(
                    out=sum4[t, hf][:],
                    lhsT=w4[:, a, 2 * P * t:2 * P * (t + 1)].bitcast(E2M1),
                    lhsT_scale=w4s[:, a, P * t:P * (t + 1)],
                    rhs=v[a][hf][:].bitcast(E4M3),
                    rhs_scale=v_sc[a][:, half(hf)],
                    start=(a == 0), stop=(a == PASSES - 1))
        read4 = {key: staged(*key) for key in order}
        for key in order:
            nc.scalar.copy(out=read4[key][:], in_=sum4[key][:])

        w1_bf = [held(f"w1_bf{a}", [P, PACK * H], BF16) for a in range(PASSES)]
        w1_q = [held(f"w1_q{a}", [P, H], U32) for a in range(PASSES)]
        w1_sc = [held(f"w1_sc{a}", [P, H], U8) for a in range(PASSES)]
        for a in range(PASSES):
            nc.vector.tensor_copy(
                out=w1_bf[a][:].rearrange("p (t m j) -> p m j t", t=PACK, j=PACK),
                in_=w1_raw[a][:].rearrange("p j (m t) -> p m j t", t=PACK))
            if a == 0:
                for t in range(PACK):
                    nc.sync.dma_start(lay_t[t][:], lay.rearrange("(p t) m -> t p m", t=PACK)[t])
            pieces = 1 if a < PASSES - 1 else 2
            width = H // pieces
            for c in range(0, H, width):
                nc.vector.quantize_mx(
                    out=w1_q[a][:, c:c + width].bitcast(E4M3),
                    scales=w1_sc[a][:, c:c + width],
                    in_=w1_bf[a][:, PACK * c:PACK * (c + width)])

        sum1 = {key: bank(*key) for key in order}

        def w1_pass(a, t, hf):
            nc.tensor.matmul_mx(
                out=sum1[t, hf][:],
                lhsT=w1_q[a][:, P * t:P * (t + 1)].bitcast(E4M3),
                lhsT_scale=w1_sc[a][:, P * t:P * (t + 1)],
                rhs=v[a][hf][:].bitcast(E4M3),
                rhs_scale=v_sc[a][:, half(hf)],
                start=(a == 0), stop=(a == PASSES - 1))

        for t, hf in order:
            w1_pass(0, t, hf)
        for step in range(PACK + 1):
            for hf in range(HALVES):
                if step == 0:
                    w1_pass(1, 0, hf)
                if step + 1 < PACK:
                    w1_pass(1, step + 1, hf)
            for hf in range(HALVES):
                if step < PACK:
                    w1_pass(2, step, hf)

        h = [held(f"h{t}", [P, S], F32) for t in range(PACK)]
        for t, hf in order:
            nc.vector.tensor_tensor(h[t][:, half(hf)], sum1[t, hf][:], read4[t, hf][:], ALU.min)

        weight = [held(f"weight{t}", [P, NP], F32) for t in range(PACK)]
        for t in range(PACK):
            nc.gpsimd.tensor_tensor(weight[t][:], lay_t[t][:], wgs_t[:, t, :], ALU.mult)

        look = [held(f"look{t}", [P, NP], F32) for t in range(PACK)]
        page = [held(f"page{t}", [P, S], F32) for t in range(PACK)]
        for t in range(PACK):
            nc.scalar.activation(
                out=look[t][:], in_=h[t][:].indirect(pos1_t[:]), func=ACT.Sigmoid, bias=thr_t[:, t:t + 1])
            nc.scalar.activation(out=page[t][:], in_=h[t][:], func=ACT.Copy, scale=skip_t[:, t:t + 1])

        page_bf = [held(f"page_bf{hf}", [P, BANK, PACK], BF16) for hf in range(HALVES)]
        for t in range(PACK):
            nc.vector.tensor_tensor(page[t][:].indirect(pos2_t[:]), look[t][:], weight[t][:], ALU.mult)
            for hf in range(HALVES):
                if hf == 0 and t >= 2:
                    nc.vector.tensor_scalar(
                        page_bf[hf][:, :, t], page[t][:, half(hf)], gain_t[:, t:t + 1], None, ALU.mult)
                else:
                    nc.scalar.activation(
                        out=page_bf[hf][:, :, t], in_=page[t][:, half(hf)], func=ACT.Copy,
                        scale=gain_t[:, t:t + 1])

        out_rows = out.rearrange("(p t) j -> t p j", t=PACK)
        page_q = [held(f"page_q{hf}", [P, BANK], U32) for hf in range(HALVES)]
        page_sc = [held(f"page_sc{hf}", [P, BANK], U8) for hf in range(HALVES)]
        for hf in range(HALVES):
            nc.vector.quantize_mx(
                out=page_q[hf][:].bitcast(E4M3), scales=page_sc[hf][:],
                in_=page_bf[hf][:].rearrange("p c t -> p (c t)"))
        for hf in range(HALVES):
            for t in range(PACK):
                acc = bank(t, hf)
                nc.tensor.matmul_mx(
                    out=acc[:],
                    lhsT=w3[:, P * t:P * (t + 1)].bitcast(E4M3),
                    lhsT_scale=w3s[:, P * t:P * (t + 1)],
                    rhs=page_q[hf][:].bitcast(E4M3),
                    rhs_scale=page_sc[hf][:],
                    start=True, stop=True)
                result = staged(t, hf)
                nc.vector.tensor_tensor(result[:], acc[:], h[t][:, half(hf)], ALU.add)
                nc.sync.dma_start(out_rows[t][:, half(hf)], result[:])
